import numpy as np, ml_dtypes
CORES = [16,17,18,19,32,33,34,35]
N = 8
BF = ml_dtypes.bfloat16
def gentries(a):
    return np.ascontiguousarray(a.reshape(8, 16, -1).transpose(0, 2, 1)).reshape(8, -1)
def gtable(e):
    e = np.asarray(e); return np.ascontiguousarray(e.reshape(8, -1, 16).transpose(0, 2, 1)).reshape(128, -1).astype(np.int32)
V, G, CAP, TH, Q, RO = 2560, 384, 64, 5, 8, 5
H = (N - 1) * G
W = V + H
def near(rng, b, m, C, L):
    k = (rng.random((N, 8, m)) * C).astype(np.int64)
    f = np.take_along_axis(np.broadcast_to(b, (N, 8, 15, 4)), k[:, :, None, :], 3) + rng.integers(-4, 5, (N, 8, 15, m))
    lev = (rng.random((N, 8, m)) * (L + 1)).astype(np.int64)
    return np.concatenate([f & 63, lev[:, :, None]], axis=2)
def parts(rng):
    b = rng.integers(0, 64, (8, 15, 4)); C = rng.integers(1, 4, (N, 8, 1)); L = rng.choice(np.array([2, 3, 5]), (N, 8, 1))
    x = near(rng, b, V, C, L); gx = near(rng, b, H, C, L); c0 = rng.integers(0, 16, (N, 8, V))
    pl = rng.integers(0, W, (N, 8, 16, V)); dr = rng.integers(0, 4, (N, 8, 16, V))
    snd = np.ascontiguousarray(np.argsort(rng.random((N, 8, N - 1, V)), axis=-1)[..., :G])
    return x, gx, c0, pl, dr, snd
def pack(x, gx, c0, pl, dr, snd):
    return {"x": np.ascontiguousarray(x.reshape(N, 128, V)).astype(np.float32).astype(BF), "nb": np.ascontiguousarray((4 * pl + dr).reshape(N, 128, V)).astype(np.int32),
            "gx": np.ascontiguousarray(gx.reshape(N, 128, H)).astype(np.float32).astype(BF), "c0": c0.astype(np.float32).astype(BF),
            "snd": np.stack([gtable(a.reshape(8, -1)) for a in snd])}
def setup_inputs(rng):
    return pack(*parts(rng))
def setup_inputs_room(rng):
    x, gx, c0, pl, dr, snd = parts(rng); u = V // 4; P = rng.integers(16, 48, (8, 15, 1)); C = np.array([0, 1, CAP - 1, CAP, CAP + 1, G])
    first = ((CAP, CAP + 1, G, CAP - 1, 1, 0, CAP, CAP + 1), (CAP, CAP + 1, G, CAP - 1, 2, 1, G, CAP + 1))
    later = (first[0], (0, 0, 1, 0, 1, 0, CAP, CAP))
    watch, slots = {}, {}
    def close(m, g):
        return P[g] + rng.integers(-1, 2, (15, m))
    for q in range(N):
        for g in range(8):
            o = rng.permutation(V); a, b, t, w = o[:u], o[u:2 * u], o[2 * u:3 * u], o[3 * u:]
            watch[q, g] = w; gx[q, g, :15] = close(H, g); gx[q, g, 15] = 1
            x[q, g, 15, a] = rng.integers(20, 64, u); x[q, g, 15, b] = 0; x[q, g, 15, t] = 1; x[q, g, 15, w] = 2
            for part in (b, t, w): x[q, g, :15][:, part] = close(len(part), g)
            pl[q, g][:, a] = b[rng.integers(0, u, (16, u))]; pl[q, g][:, t] = b[rng.integers(0, u, (16, u))]
            c0[q, g, t] = rng.integers(0, 9, u)
            for i in range(int(rng.integers(1, 3))): pl[q, g][c0[q, g, t] + i, t] = a[rng.integers(0, u, u)]
            dr[q, g][:, t] = dr[q, g][:, t] & 1; dr[q, g][:, a[:u // 2]] = 0
            for d in range(N - 1):
                n = int(rng.choice(C)); k = n if rng.random() < 0.5 else min(n, int(rng.choice(C)))
                if q < 2 and d == 0: n, k = first[q][g], later[q][g]
                kind = np.repeat(np.array([2, 1, 0]), np.array([k, n - k, G - n]))
                v = np.concatenate([rng.permutation(a)[:k], rng.permutation(t)[:n - k], rng.permutation(b)[:G - n]])
                s = rng.permutation(G); kind = kind[s]; v = v[s]
                if (q + d + g) % 2 == 0 and 0 < n <= CAP:
                    i = int(np.flatnonzero(kind)[-1]); e = np.array([i, G - 1]); kind[e] = kind[e[::-1]]; v[e] = v[e[::-1]]
                snd[q, g, d] = v; m = np.flatnonzero(kind); z = np.flatnonzero(kind == 2)
                slots[q, g, d] = np.concatenate([np.array([0, G - 1]), m[:1], m[:CAP][-1:], m[CAP:CAP + 1], z[:1], z[-1:], rng.permutation(m)[:8], rng.integers(0, G, 4)]).astype(np.int64)
    for q in range(N):
        for g in range(8):
            w = watch[q, g]; see = np.concatenate([V + d * G + slots[(q - d - 1) % N, g, d] for d in range(N - 1)])
            pl[q, g][c0[q, g, w], w] = see[np.arange(len(w)) % len(see)]
    return pack(x, gx, c0, pl, dr, snd)
def setup_inputs_ties(rng):
    x, gx, c0, pl, dr, snd = parts(rng); b = rng.integers(TH + 1, 63 - TH, (8, 15, 1))
    def edge(m):
        n = Q - 1 + rng.integers(0, 2, (N, 8, 1, m)); k = np.argsort(rng.random((N, 8, 15, m)), axis=2) < n
        root = rng.random((N, 8, 1, m)) < 0.5
        f = b + np.where(root, 0, np.where(k, TH, TH + 1) * (2 * rng.integers(0, 2, (N, 8, 15, m)) - 1))
        return np.concatenate([f, np.where(root, 0, rng.choice(np.array([1, 1, 1, 2]), (N, 8, 1, m)))], axis=2)
    return pack(edge(V), edge(H), c0, pl, dr, snd)
def setup_inputs_ends(rng):
    x, gx, c0, pl, dr, snd = parts(rng)
    c0[:, ::2] = rng.integers(14, 16, (N, 4, V)); c0[:, 1] = 0
    x[:, 2:4, 15] = rng.choice(np.array([0, 62, 62, 63]), (N, 2, V)); gx[:, 2:4, 15] = rng.choice(np.array([61, 62, 63]), (N, 2, H))
    x[:, 4, :15] = 63 * rng.integers(0, 2, (N, 15, V)); dr[:, 5] = 3
    pl[:, 1] = rng.choice(np.array([0, V - 1, V, W - 1]), (N, 16, V)); pl[:, 5] = rng.choice(np.array([0, V - 1, V, W - 1]), (N, 16, V))
    pl[:, 3] = np.arange(V); pl[:, 6] = rng.integers(V, W, (N, 16, V)); pl[:, 7] = pl[:, 7, :1]
    snd[:, ::2] = rng.choice(np.array([0, V - 1, V // 2, 3]), (N, 4, N - 1, G))
    return pack(x, gx, c0, pl, dr, snd)
def setup_inputs_still(rng):
    x, gx, c0, pl, dr, snd = parts(rng); q = rng.permutation(N); a, b = int(q[0]), int(q[1])
    few = rng.permutation(V)[None, :] < CAP // 2
    x[a, :, 15] = np.where(few, np.maximum(x[a, :, 15], 1), 0); x[b, :, 15] = rng.integers(40, 64, (8, V))
    x[:, int(rng.integers(0, 8)), 15] = 0
    return pack(x, gx, c0, pl, dr, snd)
def setup_inputs_spread(rng):
    x, gx, c0, pl, dr, snd = parts(rng)
    def cols(m):
        f = (np.exp2(6 * rng.random((N, 8, 1, m))) * rng.random((N, 8, 15, m))).astype(np.int64)
        return np.minimum(np.concatenate([f, (64 * rng.random((N, 8, 1, m)) ** 3).astype(np.int64)], axis=2), 63)
    pl = np.minimum((W * rng.random(pl.shape) ** 2).astype(np.int64), W - 1); c0 = np.minimum((16 * rng.random(c0.shape) ** 2).astype(np.int64), 15)
    return pack(cols(V), cols(H), c0, pl, dr, snd)
def check_inputs(d):
    bad = []
    for k, hi in (("x", 63), ("gx", 63), ("c0", 15)):
        a = np.asarray(d[k]).astype(np.float32)
        if not np.all((a >= 0) & (a <= hi) & (a == np.floor(a))): bad.append("numbers of " + k)
    for k, hi in (("nb", 4 * W - 1), ("snd", V - 1)):
        if np.min(d[k]) < 0 or np.max(d[k]) > hi: bad.append("range of " + k)
    return bad
def reference(x, nb, gx, c0, snd):
    own = x.astype(np.float32).astype(np.int64).reshape(N, 8, 16, V); gh = gx.astype(np.float32).astype(np.int64).reshape(N, 8, 16, H)
    cur = c0.astype(np.float32).astype(np.int64)
    e = nb.astype(np.int64).reshape(N, 8, 16, V); pl = e >> 2; dr = e & 3
    sl = np.stack([gentries(a) for a in snd]).astype(np.int64).reshape(N, 8, N - 1, G)
    root = own[:, :, 15] == 0
    for s in range(RO):
        p = np.take_along_axis(pl, cur[:, :, None], 2)
        diff = np.take_along_axis(np.concatenate([own, gh], axis=3), p, 3) - own
        votes = np.add.reduce((np.abs(diff[:, :, :15]) <= TH).astype(np.int64), axis=2)
        ok = (votes >= Q) & (diff[:, :, 15] == -1)
        moved = ~ok & ~root
        f, lev = own[:, :, :15], own[:, :, 15]
        f = np.where(ok[:, :, None], f + np.clip(diff[:, :, :15], -1, 1), np.where(moved[:, :, None], (f + dr[:, :, :15]) & 63, f))
        lev = np.where(moved & (cur == 15), np.minimum(lev + 1, 63), lev)
        cur = np.where(moved, (cur + 1) & 15, cur)
        own = np.concatenate([f, lev[:, :, None]], axis=2)
        if s == RO - 1: break
        for a in range(N):
            for t in range(1, N):
                q = (a - t) % N; ix = sl[q, :, t - 1]
                m = np.take_along_axis(moved[q], ix, 1).astype(np.int64); before = np.add.accumulate(m, axis=1) - m
                come = ((m == 1) & (before < CAP))[:, None, :]
                v = np.take_along_axis(own[q], ix[:, None, :], 2)
                gh[a, :, :, (t - 1) * G:t * G] = np.where(come, v, gh[a, :, :, (t - 1) * G:t * G])
    return {"yx": own.reshape(N, 128, V).astype(np.float32).astype(BF), "yc": cur.astype(np.float32)}

import numpy as np
from concourse.bass import DstId, RemoteDMATransfer
from concourse.mybir import AluOpType as A, ActivationFunctionType as AF

N, V, G, H, RO = 8, 2560, 384, 2688, 5
CH, NC = 512, 5
K = 32768
M32 = 402653184.0
M16 = 201326592.0
PW = 68
CUTV, CUTA = [0, 6, 10], [10, 16, 21]
RA = 8
RH = 256
PIECES = ((0, 1536), (1536, V))
YP = ((0, 2048), (2048, V))
Y0 = ((0, 1024), (1024, V))
ZB = ["pb0", "pb1", "pt", "pb0", "pb1"]
CY, PE, GA, SC, OV, HOP, FAR, NEAR = 1.04, 0.52, 1.56, 3.8, 50, 160, 5200, 4000
YT = (1000, 3500)
ROUNDS, NOISE = 400, 250
MATS = ["WC0", "WT", "WB", "WI", "WD", "ID", "WY", "WW", "WV", "WS", "NI", "W3", "WZ", "WK", "UT", "IND", "CA"]
MI = {n: i for i, n in enumerate(MATS)}


def _sb(cols, dtype):
    return ("sbuf", [128] + (cols if isinstance(cols, list) else [cols]), dtype)


SCRATCH = {"cm": _sb([8 * len(MATS), 16], "bfloat16"), "hi": _sb([21, 8], "bfloat16"),
           "eb": _sb([21, 4, 8], "bfloat16"), "lt": _sb([21, 4, 8], "bfloat16")}
for _n, _c in (("ones", 128), ("cst", 168), ("cw", 144), ("sel", 8), ("mk", 224), ("ct", V), ("ct2", V), ("xs", V),
               ("gs", H), ("c0c", 160), ("win", V + H + 128 * 28), ("dr", V), ("dd", V), ("band", V), ("ss", V), ("st0", V),
               ("st1", V), ("qq", V), ("ff", V), ("ww", V), ("wb", V), ("yg", H + 16), ("mt", 168), ("lo", 168), ("rb", H),
               ("pv", 448), ("yy", V), ("xo", V)):
    SCRATCH[_n] = _sb(_c, "bfloat16")
for _n, _c in (("wrapb", 144), ("rs", 224), ("thr", 28), ("dlt", 28), ("col", 16), ("mcol", 4), ("z", V), ("rr", V), ("sc", 224),
               ("t1", 28), ("t2", 28), ("t3", 28), ("gp", 160), ("cur", 160)):
    SCRATCH[_n] = _sb(_c, "float32")
for _n, _c in (("pi", 4), ("nbs", V), ("d32", V), ("sn", 168), ("nd", 160), ("nx", 160), ("ns", 160), ("pp", 160),
               ("ci", 160), ("cj", 160)):
    SCRATCH[_n] = _sb(_c, "int32")
for _n, _c in (("snu", 168), ("gu", 28), ("offu", 160)):
    SCRATCH[_n] = _sb(_c, "uint16")
for _s in range(RO - 1):
    SCRATCH["pay%d" % _s] = _sb([N - 1, PW], "uint16")
    SCRATCH["land%d" % _s] = _sb((N - 1) * PW, "uint16")
BANKS = ["pa0", "pa1", "pb0", "pb1", "py0", "py1", "pt", "pw"]
for _b in BANKS:
    SCRATCH[_b] = ("psum", [128, 512], "float32")
NDMA = 50
SEMAPHORES = (["eP", "eV", "eA", "eG", "sent"] + ["d%d" % i for i in range(NDMA)]
              + ["near%d" % s for s in range(RO - 1)] + ["far%d" % s for s in range(RO - 1)])
ORDERS = {}


def routes(T, topo, rank):
    src = T.cores[rank]
    dsts = [T.cores[(rank + d) % N] for d in range(1, N)]
    far = [c for c in dsts if topo.chip(c) != topo.chip(src)]
    near = [c for c in dsts if topo.chip(c) == topo.chip(src)]
    fe = topo.engines(src, far[0])
    ne = [e for e in topo.engines(src, near[0]) if e not in fe]
    out = {}
    for cs, es in ((far, fe), (near, ne)):
        left = list(es)
        for i, c in enumerate(cs):
            n = 1
            while 2 * n <= len(left) // (len(cs) - i):
                n *= 2
            out[c] = left[:n]
            left = left[n:]
    return [(c, out[c], c in near) for c in dsts]


def place_calls(ops, pre, seq):
    st, busy = {}, {}
    for i in seq:
        t = max([0.0] + [st[j] + lat for j, lat in pre[i]])
        iv = busy.setdefault(ops[i]["eng"], [])
        lo, hi = 0, len(iv)
        while lo < hi:
            m = (lo + hi) // 2
            if iv[m][1] <= t:
                lo = m + 1
            else:
                hi = m
        while lo < len(iv) and iv[lo][0] < t + ops[i]["t"]:
            t = max(t, iv[lo][1])
            lo += 1
        iv.insert(lo, (t, t + ops[i]["t"]))
        st[i] = t
    return st, max(st[i] + ops[i]["t"] for i in seq)


def by_key(key, pre, suc):
    left = [len(p) for p in pre]
    h = [(key[i], i) for i in range(len(key)) if left[i] == 0]
    out = []
    while h:
        x = min(h)
        h.remove(x)
        out.append(x[1])
        for j, lat in suc[x[1]]:
            left[j] -= 1
            if left[j] == 0:
                h.append((key[j], j))
    return out


def order_calls(ops):
    n = len(ops)
    fw = [list(o["pre"].items()) for o in ops]
    sig = tuple((o["eng"], o["t"], tuple(f)) for o, f in zip(ops, fw))
    if sig in ORDERS:
        return ORDERS[sig]
    bw = [[] for _ in ops]
    for i in range(n):
        for j, lat in fw[i]:
            bw[j].append((i, ops[i]["t"] + lat - ops[j]["t"]))
    pr = [0.0] * n
    for i in range(n - 1, -1, -1):
        pr[i] = ops[i]["t"] + max([0.0] + [lat - ops[k]["t"] + pr[k] for k, lat in bw[i]])
    rng = np.random.RandomState(1)
    best, key = None, [-p for p in pr]
    for it in range(ROUNDS):
        st, end = place_calls(ops, fw, by_key(key, fw, bw))
        if best is None or end < best[0]:
            best = (end, st)
        base = best[1] if it % 4 == 3 else st
        e = rng.uniform(-NOISE, NOISE, n)
        sb, end = place_calls(ops, bw, by_key([-(base[i] + ops[i]["t"]) + e[i] for i in range(n)], bw, fw))
        key = [-(sb[i] + ops[i]["t"]) for i in range(n)]
    ORDERS[sig] = sorted(range(n), key=lambda i: (best[1][i], i))
    return ORDERS[sig]


def rank_program(g, core, T, topo):
    rank = T.rank_of(core)
    if rank is None:
        return
    Q = {"P": g.tensor, "V": g.vector, "A": g.scalar, "G": g, "S": g.sync}
    ops, acc, ndma, lastdma = [], {}, [0], {}

    def op(eng, fn, t, r=(), w=(), dma=0, ext=None, after=None):
        i = len(ops)
        deps, pre = set(), {}
        both = [((a, 0, 1 << 30) if isinstance(a, str) else a) + (wr,) for lst, wr in ((r, False), (w, True)) for a in lst]
        for name, lo, hi, wr in both:
            ps = name in BANKS
            for (j, l2, h2, w2) in acc.get(name, ()):
                if l2 >= hi or lo >= h2 or not (w2 or wr or ps):
                    continue
                if ops[j]["eng"] == eng and not ops[j]["dma"] and not dma and (eng == "P" or not (wr or w2)):
                    pre.setdefault(j, ops[j]["t"])
                else:
                    deps.add(j)
                    pre[j] = ops[j]["t"] + HOP + ops[j]["dma"]
        for name, lo, hi, wr in both:
            if wr or name in BANKS:
                acc[name] = [x for x in acc.get(name, ()) if not (lo <= x[1] and x[2] <= hi)]
            acc.setdefault(name, []).append((i, lo, hi, wr))
        o = {"eng": eng, "fn": fn, "deps": deps, "pre": pre, "dma": dma, "ext": ext, "need": False, "t": t}
        if after:
            pre[after[0]] = after[1]
        if dma:
            o["sem"] = "d%d" % ndma[0]
            ndma[0] += 1
            if eng in lastdma and ndma[0] < 13:
                pre.setdefault(lastdma[eng], t)
            lastdma[eng] = i
        ops.append(o)
        return i

    def emit():
        order = order_calls(ops)
        pos = {j: k for k, j in enumerate(order)}
        seen = {e: {} for e in Q}
        for i in order:
            o = ops[i]
            best = {}
            for j in o["deps"]:
                k = ops[j]["sem"] if ops[j]["dma"] else ops[j]["eng"]
                if k not in best or pos[j] > pos[best[k]]:
                    best[k] = j
            o["wait"] = {}
            for k, j in best.items():
                if seen[o["eng"]].get(k, -1) < pos[j]:
                    seen[o["eng"]][k] = pos[j]
                    o["wait"][k] = j
                    ops[j]["need"] = True
        cnt = {e: 0 for e in Q}
        for i in order:
            o = ops[i]
            q = Q[o["eng"]]
            for k, j in o["wait"].items():
                if ops[j]["dma"]:
                    q.wait_ge(T.sem[k], 16)
                else:
                    q.wait_ge(T.sem["e" + k], ops[j]["n"])
            if o["ext"]:
                q.wait_ge(T.sem[o["ext"][0]], o["ext"][1])
            ins = o["fn"](q)
            if o["dma"]:
                ins.then_inc(T.sem[o["sem"]], 16)
            elif o["need"]:
                cnt[o["eng"]] += 1
                o["n"] = cnt[o["eng"]]
                ins.then_inc(T.sem["e" + o["eng"]], 1)
        return cnt

    def ck(name, c):
        return (name, c * CH, (c + 1) * CH)

    def cs(name, c):
        return T[name][:, c * CH:(c + 1) * CH]

    def mat(n, k=128):
        return T.cm[0:k, 8 * MI[n]:8 * MI[n] + 8, :]

    def mr(n):
        return ("cm", MI[n], MI[n] + 1)

    def vt(cyc):
        return OV + CY * max(64, cyc)

    def mm(bank, lo, hi, lhsT, rhs, start, stop, r, n=None):
        op("P", lambda q: q.matmul(T[bank][:, lo:hi], lhsT, rhs, start, stop), PE * (n or max(64, hi - lo)), r=r, w=[bank])

    def mmc(bank, m, name, c, start, stop, k=128):
        mm(bank, 0, CH, mat(m, k), T[name][0:k, c * CH:(c + 1) * CH], start, stop, [mr(m), ck(name, c)])

    def ts(n, out, in0, s1, s2, o0, o1, r, w):
        if o1 is None:
            op("V", lambda q: q.tensor_scalar(out, in0, s1, None, o0), vt(n), r=r, w=w)
        else:
            op("V", lambda q: q.tensor_scalar(out, in0, s1, s2, o0, o1), vt(n), r=r, w=w)

    def tt(n, out, in0, in1, o, r, w):
        op("V", lambda q: q.tensor_tensor(out, in0, in1, o), vt(n), r=r, w=w)

    def cp(n, out, in_, r, w, ext=None, after=None):
        return op("V", lambda q: q.tensor_copy(out, in_), vt(n), r=r, w=w, ext=ext, after=after)

    def ms(n, ap, val, w):
        op("V", lambda q: q.memset(ap, val), vt(n), w=w)

    def act(n, out, in_, f, r, w, bias=0.0, scale=1.0):
        op("A", lambda q: q.activation(out, in_, f, bias=bias, scale=scale), vt(n) + 15, r=r, w=w)

    def dma(eng, lat, out, in_, r=(), w=()):
        op(eng, lambda q: q.dma_start(out, in_), 60, r=r, w=w, dma=lat)

    def asel(n, ap, pat, cmp, fill, base, mul, rw):
        op("G", lambda q: q.affine_select(ap, ap, pat, cmp, fill, base, mul), 210 + 2 * CY * n, r=[rw], w=[rw])

    def iota(n, ap, pat, base, mul, w, flag=True):
        if flag:
            op("G", lambda q: q.iota(ap, pat, base, mul, allow_small_or_imprecise_dtypes=True), 160 + 2 * CY * n, w=[w])
        else:
            op("G", lambda q: q.iota(ap, pat, base, mul), 160 + 2 * CY * n, w=[w])

    def sub(n, o0, o1, k=128):
        return T.cm[0:k, 8 * MI[n]:8 * MI[n] + 8, o0:o1]

    def row(n, i, o0, o1, val):
        asel(8 * (o1 - o0), sub(n, o0, o1), [[-16, 8], [0, o1 - o0]], A.not_equal, val, -i, 1, mr(n))

    def diag(n, sh, o0, o1, val):
        asel(8 * (o1 - o0), sub(n, o0, o1), [[-16, 8], [-1, o1 - o0]], A.not_equal, val, -o0 - sh, 1, mr(n))

    def rows_from(n, i, o0, o1, val):
        asel(8 * (o1 - o0), sub(n, o0, o1), [[16, 8], [0, o1 - o0]], A.is_gt, val, i, -1, mr(n))

    def grp(n, p0, o0, o1, val, k):
        asel(8 * (o1 - o0), sub(n, o0, o1, k), [[-1, 8], [0, o1 - o0]], A.not_equal, val, -p0, 1, mr(n))

    dma("S", 2000, T.ct[2:10, :], T.c0[:, :], w=[("ct", 1, 2)])
    dma("A", 2200, T.ct[10:18, :], T.x[15:128:16, :], w=[("ct", 2, 3)])
    dma("A", 2400, T.ct[18:26, :], T.x[15:128:16, :], w=[("ct", 3, 4)])
    for c in range(NC):
        dma("S", 3000 + 900 * c, cs("nbs", c), T.nb[:, c * CH:(c + 1) * CH], w=[ck("nbs", c)])
    dma("S", 9000, T.xs[:, :], T.x[:, :], w=["xs"])
    dma("S", 11200, T.gs[:, :], T.gx[:, :], w=["gs"])
    dma("S", 11500, T.sn[:, :], T.snd[:, :], w=["sn"])
    dma("S", 11700, T.c0c[:, :], T.c0[:, :], w=["c0c"])

    ms(192, T.cm[:, 0:24, :], 0.0, [("cm", 0, 3)])
    ms(4, T.mcol[:, :], 1.0, ["mcol"])
    ms(1280, T.ct[0:2, :], 2.0, [("ct", 0, 1)])
    ms(256, T.cm[:, 24:56, :], 0.0, [("cm", 3, 7)])
    ms(576, T.cm[:, 64:, :], 0.0, [("cm", 8, 99)])
    ms(144, T.wrapb[:, :], 0.0, ["wrapb"])
    ms(72, T.cw[:, :], 0.0, ["cw"])
    ms(8, T.sel[:, :], 0.0, ["sel"])
    iota(128, T.cm[0:1, 0:8, :], [[0, 8], [-2, 16]], -1, 0, mr("WC0"))
    grp("WC0", 2, 0, 16, 4.0, 10)
    asel(1, T.mcol[0:32, 0:1], [[0, 1]], A.is_gt, 99.0, -9, 1, "mcol")
    asel(1, T.mcol[0:32, 0:1], [[0, 1]], A.is_gt, 99.0, 18, -1, "mcol")
    iota(1, T.mcol[0:32, 1:2], [[0, 1]], 62, 0, "mcol")
    asel(1, T.mcol[0:32, 1:2], [[0, 1]], A.is_gt, 0.0, -17, 1, "mcol")
    iota(128, T.cm[0:1, 8:16, :], [[0, 8], [K // 2, 16]], 4 * K, 0, mr("WT"))
    grp("WT", 2, 0, 16, -float(K), 10)
    asel(128, sub("WT", 0, 16, 10), [[0, 8], [0, 16]], A.not_equal, 2.0, -1, 1, mr("WT"))
    diag("WB", 0, 0, 16, 8.0 * K)
    iota(48, sub("WI", 6, 12, 1), [[0, 8], [2, 6]], -95, 0, mr("WI"))
    iota(48, sub("WI", 0, 6, 1), [[0, 8], [0, 6]], -1, 0, mr("WI"))
    iota(32, sub("WI", 12, 16, 1), [[0, 8], [2, 4]], -1, 0, mr("WI"))
    grp("WI", 2, 6, 12, 4.0, 18)
    grp("WI", 10, 6, 12, 128.0, 18)
    grp("WI", 10, 12, 13, 4.0, 18)
    grp("WI", 18, 6, 12, -128.0, 26)
    asel(48, sub("WI", 6, 12, 26), [[0, 8], [0, 6]], A.not_equal, 3968.0, -1, 1, mr("WI"))
    iota(1, T.pi[:, 0:1], [[0, 1]], 0, 1, "pi", False)
    asel(8, T.wrapb[:, 15:143:16], [[16, 8]], A.is_gt, 1.0, 0, -1, "wrapb")
    asel(8, T.wrapb[:, 15:143:16], [[16, 8]], A.is_gt, 0.0, 16, -1, "wrapb")
    grp("WD", 10, 0, 15, 3.0, 18)
    diag("ID", 0, 0, 16, 1.0)
    row("WY", 7, 15, 16, 1.5)
    row("WY", 6, 15, 16, -1.5)
    rows_from("WV", 0, 0, 11, -1.0)
    rows_from("WV", 15, 0, 11, -16.0)
    rows_from("WV", 16, 0, 11, 0.0)
    diag("WS", 0, 1, 13, 64.0)
    diag("WS", -1, 2, 6, 32.0)
    row("WS", 12, 1, 2, 32.0)
    diag("WS", 1, 6, 11, 32.0)
    row("WS", 13, 0, 1, 23.5)
    row("WS", 13, 1, 11, 55.5)
    row("WS", 13, 13, 16, 1.0)
    row("WZ", 0, 0, 16, 256.0)
    row("WZ", 13, 0, 16, 256.0)
    asel(8, T.sel[:, :], [[-16, 8]], A.not_equal, 1.0, -15, 1, "sel")
    asel(128, mat("UT"), [[-16, 8], [-1, 16]], A.is_gt, 1.0, 0, 1, mr("UT"))
    grp("IND", 0, 0, 16, 1.0, 8)
    iota(224, T.mk[0:8, :], [[2 * G, 7], [0, 32]], 0, 0, "mk")
    asel(224, T.mk[0:8, :], [[0, 28], [-1, 8]], A.is_equal, -2048.0, 0, 1, "mk")
    iota(28, T.thr[:, :], [[2 * G, 7], [0, 4]], 2 * G, 0, "thr")
    iota(28, T.dlt[:, :], [[8 - 2 * G, 7], [2, 4]], 2 * (H - G), 56, "dlt")
    rows_from("WK", 1, 0, 16, K / 2.0)
    rows_from("WK", 6, 0, 16, 0.0)
    row("WK", 13, 0, 16, 3.5 * K)
    cwv = T.cw[:, 15:143:16]
    asel(8, cwv, [[16, 8]], A.is_gt, 0.5, 1, -1, "cw")
    asel(8, cwv, [[16, 8]], A.is_gt, 0.0, 6, -1, "cw")
    asel(8, cwv, [[-16, 8]], A.not_equal, 2.5, -13, 1, "cw")
    ms(32, sub("CA", 15 - RA, 15), 1.0, [mr("CA")])
    ms(64, T.ones[:, :], 1.0, ["ones"])
    ms(84, T.cst[:, :], -7.5 / 128, ["cst"])
    ms(8, T.yg[:, H:], 0.0, [("yg", H, H + 16)])
    ms(84, T.rb[:, 15:H:16], 2.0, [("rb", 15, 16)])
    ms(84, T.lt[:, :, 0, :], 0.0, [("lt", 0, 1)])
    ms(224, T.rs[:, :], 1.0, ["rs"])
    ms(28, T.rs[:, 0:224:8], 0.0, ["rs"])
    ts(1, T.pi[:, 2:3], T.pi[:, 0:1], 15, None, A.bitwise_and, None, ["pi"], ["pi"])
    ts(1, T.col[:, 0:1], T.pi[:, 2:3], 15.0, M32, A.not_equal, A.mult, ["pi"], ["col"])
    ts(1, T.col[:, 8:9], T.pi[:, 2:3], 15.0, -96.0, A.not_equal, A.mult, ["pi"], ["col"])
    ts(1, T.col[:, 4:5], T.col[:, 0:1], 3.0, None, A.max, None, ["col"], ["col"])
    ts(64, mat("NI"), mat("ID"), -1.0, None, A.mult, None, [mr("ID")], [mr("NI")])
    ts(64, mat("WW"), mat("ID"), T.col[:, 8:9], None, A.mult, None, [mr("ID"), "col"], [mr("WW")])
    ts(64, mat("W3"), mat("WW"), 1.0 / 32, None, A.mult, None, [mr("WW")], [mr("W3")])

    pa, pb, py = ["pa0", "pa1"], ["pb0", "pb1"], ["py0", "py1"]

    def wrap(a, b, bank):
        for r in range(16):
            mm(bank, a // 16, b // 16, T.wrapb[:, 15 - r:143 - r], T.rr[:, a + r:b:16], r == 0, r == 15,
               ["wrapb", ("rr", a, b)], 4 * max(64, (b - a) // 16))

    def fail_values(st, first):
        for a, b in YP:
            dma("S", 3200, T.win[:, a:b], T.xo[:, a:b], r=[("xo", a, b)], w=[("win", a, b)])
        if not first:
            dma("S", 4000, T.yy[:, :], T.dr[:, :], r=["dr"], w=["yy"])
        add = "dr" if first else "xo"
        for a, b in (Y0 if first else YP):
            op("G", lambda q, a=a, b=b: q.dma_start(T.yy[:, a:b], T[add][:, a:b], accum_op=A.add), YT[0],
               r=[(add, a, b), ("yy", a, b)], w=[("yy", a, b)], dma=YT[1])
        for c in range(NC):
            b = py[c % 2]
            act(CH, cs("ww", c), cs("yy", c), AF.Sign, [ck("yy", c)], [ck("ww", c)], bias=-190.5)
            mmc(b, "WY", st, c, True, False)
            mmc(b, "ID", "yy", c, False, False)
            mmc(b, "WW", "ww", c, False, True)
            act(CH, cs("ff", c), T[b][:, :], AF.Identity, [b, "col"], [ck("ff", c)], bias=T.col[:, 8:9])

    def places(a, b):
        ts(b - a, T.pp[:, a:b], T.ns[:, a:b], 2, 8191, A.arith_shift_right, A.bitwise_and, [("ns", a, b)], [("pp", a, b)])
        cp(b - a, T.offu[:, a:b], T.pp[:, a:b], [("pp", a, b)], [("offu", a, b)])

    def look(st, keep):
        for c in range(NC):
            b = pa[c % 2]
            mmc(b, "WK", st, c, True, True)
            for a in range(0, CH, RH):
                o = c * CH + a
                tt(RH, T.rr[:, o:o + RH], T[b][:, a:a + RH], T.z[:, o:o + RH], A.min, [b, ck("z", c)], [("rr", o, o + RH)])
        for a, b in PIECES:
            wrap(a, b, "pw")
        tt(160, T.nd[:, :], T.pw[:, 0:160], T.gp[:, :], A.subtract, ["gp", "pw"], ["nd"])
        if keep:
            ts(160, T.gp[:, :], T.pw[:, 0:160], 4.0, None, A.add, None, ["pw"], ["gp"])
        ts(160, T.nx[:, :], T.nd[:, :], 16 * K - 1, None, A.bitwise_and, None, ["nd"], ["nx"])
        tt(320, T.ns[:, :], T.ns[:, :], T.nx[:, :], A.min, ["ns", "nx"], ["ns"])
        places(0, 160)

    ctr = [("ct", 0, 2)]
    for c in range(NC):
        mm(pa[c % 2], 0, CH, mat("WC0", 10), T.ct[0:10, c * CH:(c + 1) * CH], True, True, [mr("WC0")] + ctr)
        act(CH, cs("wb", c), T[pa[c % 2]][:, :], AF.Sign, [pa[c % 2]], [ck("wb", c)])
        mm(pb[c % 2], 0, CH, mat("WT", 10), T.ct[0:10, c * CH:(c + 1) * CH], True, False, [mr("WT")] + ctr)
        mmc(pb[c % 2], "WB", "wb", c, False, True)
        tt(CH, cs("z", c), T[pb[c % 2]][:, :], cs("nbs", c), A.add, [pb[c % 2], ck("nbs", c)], [ck("z", c)])
        act(CH, cs("rr", c), cs("z", c), AF.Relu, [ck("z", c)], [ck("rr", c)], bias=float(K), scale=-1.0)
        ts(CH, cs("d32", c), cs("nbs", c), 3, None, A.bitwise_and, None, [ck("nbs", c)], [ck("d32", c)])
        ts(CH / 2, T.ct2[0:26, c * CH:(c + 1) * CH], T.ct[0:26, c * CH:(c + 1) * CH], T.mcol[0:26, 0:1], T.mcol[0:26, 1:2],
           A.min, A.max, ["ct", "mcol"], [ck("ct2", c)])
    for a, b in Y0:
        ts((b - a) / 2, T.xo[:, a:b], T.xs[:, a:b], 3.0, None, A.mult, None, ["xs"], [("xo", a, b)])
        ts((b - a) / 2, T.yy[:, a:b], T.xs[:, a:b], 3.0, None, A.mult, None, ["xs"], [("yy", a, b)])
    for (a, b), bank in zip(((0, 1024), (1024, V)), ("pw", "pt")):
        wrap(a, b, bank)
        a, b = a // 16, b // 16
        ts(b - a, T.ns[:, a:b], T[bank][:, a:b], -1.0, 16.0 * K - 4, A.mult, A.add, [bank], [("ns", a, b)])
        places(a, b)
    ts(160, T.gp[:, :], T.ns[:, :], 8.0, None, A.add, None, ["ns"], ["gp"])
    for c in range(NC):
        mmc(py[c % 2], "WD", "ct2", c, True, True, 18)
        tt(CH, cs("dr", c), T[py[c % 2]][:, :], cs("d32", c), A.mult, [py[c % 2], ck("d32", c)], [ck("dr", c)])
    for c in range(NC):
        mmc(pb[c % 2], "WI", "ct2", c, True, True, 26)
        act(CH, cs("st1", c), T[pb[c % 2]][:, :], AF.Sign, [pb[c % 2]], [ck("st1", c)])
    for a in range(0, H, 896):
        ts(448, T.win[:, V + a:V + a + 896], T.gs[:, a:a + 896], 3.0, None, A.mult, None, ["gs"], [("win", V + a, V + a + 896)])
    cp(168, T.snu[:, :], T.sn[:, :], ["sn"], ["snu"])
    fail_values("st1", True)

    rt = routes(T, topo, rank)
    sent = 0
    for s in range(RO):
        sp, sn_ = "st%d" % ((s + 1) % 2), "st%d" % (s % 2)
        last = s == RO - 1
        for c in range(NC):
            a, b = pa[c % 2], ZB[c]
            tt(GA * CH, cs("dd", c), T.win[:, 0:V + H].indirect(T.offu[:, 32 * c:32 * c + 32]), cs("xo", c), A.subtract,
               [("win", 0, V + H), ("offu", 32 * c, 32 * c + 32), ck("xo", c)], [ck("dd", c)])
            act(CH, cs("ss", c), cs("dd", c), AF.Sign, [ck("dd", c)], [ck("ss", c)])
            mmc(a, "WS", sp, c, True, False)
            ts(CH / 2, cs("band", c), cs("dd", c), T.col[:, 4:5], T.col[:, 0:1], A.add, A.is_equal, [ck("dd", c), "col"], [ck("band", c)])
            mmc(a, "WV", "band", c, False, True)
            act(CH, cs(sn_, c), T[a][:, :], AF.Sign, [a], [ck(sn_, c)])
            mmc(b, "NI", "xo", c, True, False)
            mmc(b, "W3", "ss", c, False, False)
            mmc(b, "WZ", sn_, c, False, True)
            tt(CH, cs("qq", c), T[b][:, :], cs("ff", c), A.min, [b, ck("ff", c)], [ck("qq", c)])
            if last:
                act(CH, cs("xs", c), cs("qq", c), AF.Abs, [ck("qq", c)], [ck("xs", c)], scale=1.0 / 3)
                dma("S", 2500, T.yx[:, c * CH:(c + 1) * CH], cs("xs", c), r=[ck("xs", c)], w=[("yx", c, c + 1)])
            else:
                act(CH, cs("xo", c), cs("qq", c), AF.Abs, [ck("qq", c)], [ck("xo", c)])
        if last:
            for q_ in range(16):
                mm("pw", 0, 160, T.cw[:, 15 - q_:143 - q_], T[sn_][:, 160 * q_:160 * q_ + 160], q_ == 0, q_ == 15,
                   ["cw", (sn_, 160 * q_, 160 * q_ + 160)])
            tt(160, T.ci[:, :], T.pw[:, 0:160], T.c0c[:, :], A.add, ["pw", "c0c"], ["ci"])
            ts(160, T.cj[:, :], T.ci[:, :], 15, None, A.bitwise_and, None, ["ci"], ["cj"])
            cp(160, T.cur[:, :], T.cj[:, :], ["cj"], ["cur"])
            dma("A", 2300, T.yc[:, :], T.cur[:, :], r=["cur"], w=["yc"])
            break

        for k in range(max(len(CUTV), len(CUTA)) - 1):
            for cut in (CUTV, CUTA):
                if k + 1 >= len(cut):
                    continue
                a, b = cut[k], cut[k + 1]
                src, dst = T.qq[:, :].indirect(T.snu[:, 8 * a:8 * b]), T.yg[:, 128 * a:128 * b]
                if cut is CUTV:
                    cp(GA * 128 * (b - a), dst, src, ["qq", "snu"], [("yg", 128 * a, 128 * b)])
                else:
                    act(GA * 128 * (b - a), dst, src, AF.Copy, ["qq", "snu"], [("yg", 128 * a, 128 * b)])
                for u in range(a, b):
                    d, j = divmod(u, 3)
                    mm("pt", j * 56 + d * 8, j * 56 + d * 8 + 8, T.yg[:, 128 * u:128 * u + 128], T.sel[:, :], True, True,
                       [("yg", 128 * u, 128 * u + 128), "sel"])
        mm("pw", 0, 168, T.ones[:, :], T.cst[:, :], True, False, ["ones", "cst"])
        ts(168, T.mt[:, :], T.pt[:, 0:168], 0.5, None, A.is_gt, None, ["pt"], ["mt"])
        mm("pw", 0, 168, mat("UT"), T.mt[:, :], False, False, [mr("UT"), "mt"])
        mm("pw", 56, 168, T.ones[:, :], T.mt[:, 0:112], False, False, ["ones", "mt"])
        mm("pw", 112, 168, T.ones[:, :], T.mt[:, 0:56], False, True, ["ones", "mt"])
        mm("pt", 0, 224, mat("IND", 8), T.mk[0:8, :], True, False, [mr("IND"), "mk"])
        ts(168, T.hi[:, :, :], T.pw[:, 0:168], M16, M16, A.add, A.subtract, ["pw"], ["hi"])
        tt(168, T.lo[:, :], T.pw[:, 0:168], T.hi[:, :, :], A.subtract, ["pw", "hi"], ["lo"])
        for r in range(14, -1, -1):
            if r < 15 - RA:
                ts(84, T.rb[:, r:H:16], T.lo[:, :], r - 7.25, 2.0, A.is_le, A.mult, ["lo"], [("rb", r, r + 1)])
            else:
                act(168, T.rb[:, r:H:16], T.lo[:, :], AF.Sign, ["lo"], [("rb", r, r + 1)], bias=r - 7.25, scale=-1.0)
        for t in range(4):
            ts(84, T.eb[:, :, t, :], T.hi[:, :, :], 16.0 * t, None, A.is_equal, None, ["hi"], [("eb", t, t + 1)])
        for t in range(1, 4):
            ts(84, T.lt[:, :, t, :], T.hi[:, :, :], 16.0 * t, 2.0, A.is_lt, A.mult, ["hi"], [("lt", t, t + 1)])
        for j in range(3):
            mm("pt", 0, 224, mat("CA"), T.eb[:, 7 * j:7 * j + 7, :, :], False, False, [mr("CA"), "eb"])
            mm("pt", 0, 224, T.ones[:, :], T.lt[:, 7 * j:7 * j + 7, :, :], False, False, ["ones", "lt"])
        for u in range(21):
            d = u % 7
            mm("pt", 32 * d, 32 * d + 32, T.rb[:, 128 * u:128 * u + 128], T.eb[:, u, :, :], False, u == 20, ["rb", "eb"])
        pay, land = "pay%d" % s, "land%d" % s
        op("V", lambda q: q.tensor_tensor_scan(T.sc[:, :], T.rs[:, :], T.pt[:, 0:224], 0.0, A.mult, A.max), vt(224), r=["rs", "pt"], w=["sc"])
        gi = T.sc[:, 7:224:8]
        ts(28, T.gu[:, :], gi, 0.5, None, A.mult, None, ["sc"], ["gu"])
        act(GA * 448, T.pv[:, :], T.yg[:, :].indirect(T.gu[:, :]), AF.Copy, ["yg", "gu"], ["pv"])
        tt(56, T.t1[:, :], gi, T.thr[:, :], A.is_ge, ["sc", "thr"], ["t1"])
        tt(56, T.t2[:, :], T.t1[:, :], T.dlt[:, :], A.mult, ["t1", "dlt"], ["t2"])
        tt(56, T.t3[:, :], T.t2[:, :], gi, A.add, ["t2", "sc"], ["t3"])
        ts(28, T[pay][:, :, 64:68], T.t3[:, :], 0.5, None, A.mult, None, ["t3"], [(pay, 1, 2)])
        cp(224, T[pay][:, :, 0:64], T.pv[:, :], ["pv"], [(pay, 0, 1)])

        def send(q, s=s, pay=pay, land=land):
            trs = []
            for d, (c, es, near) in enumerate(rt):
                rid, pid, _e = topo.addr(c)
                trs.append(RemoteDMATransfer(dst_ids=[DstId(rid=rid, pnc=pid)], dma_engine_mask=sum(1 << e for e in es),
                                             remote_sem=T.sem[("near%d" if near else "far%d") % s],
                                             src=T[pay][:, d, :], dst=T[land][:, PW * d:PW * d + PW]))
            return q.remote_dma_fused(trs, local_sem=T.sem.sent)
        si = op("G", send, 300, r=[pay])
        sent += sum(len(es) for c, es, near in rt)

        fail_values(sn_, False)
        look(sn_, s < RO - 2)
        for near in (True, False):
            src = [(d, routes(T, topo, (rank - d - 1) % N)[d]) for d in range(N - 1)]
            src = [(d, len(x[1])) for d, x in src if x[2] == near]
            ext = (("near%d" if near else "far%d") % s, sum(n for d, n in src))
            aft = (si, NEAR if near else FAR)
            for d, n in src:
                cp(SC * 64, T.win[:, V:].indirect(T[land][:, PW * d + 64:PW * d + 68]), T[land][:, PW * d:PW * d + 64],
                   [], [("win", V, 1 << 20)], ext, aft)
                ext = None

    op("G", lambda q: q.wait_ge(T.sem.sent, sent), 10, r=["yx", "yc"])
    cnt = emit()
    for e in "PVAG":
        if cnt[e]:
            g.wait_ge(T.sem["e" + e], cnt[e])
